import numpy as np
import ml_dtypes


def mxq(x, axis, fmt="e4m3"):
    dtype, down = {"e4m3": (ml_dtypes.float8_e4m3fn, 7), "e5m2": (ml_dtypes.float8_e5m2, 14)}[fmt]
    v = np.moveaxis(np.asarray(x, np.float32).astype(ml_dtypes.bfloat16).astype(np.float64), axis, -1)
    blocks = v.reshape(v.shape[:-1] + (-1, 32))
    amax = np.abs(blocks).max(-1, keepdims=True)
    byte = np.maximum(np.where(amax > 0, np.frexp(amax)[1] - 1 + 127, 0) - down, 1)
    scale = np.exp2(byte - 127.0)
    codes = (blocks / scale).astype(np.float32).astype(dtype).astype(np.float64)
    return np.moveaxis((codes * scale).reshape(v.shape), -1, axis)


WIDE = False


def mx_kscale(k):
    if not WIDE:
        return np.ones(k)
    levels = np.array([24, -24, 12, -12, 0])
    if k % 512:
        return np.exp2(np.random.permutation(np.resize(levels, k // 32))).repeat(32)
    a = np.empty((k // 512, 16))
    for p in range(k // 512):
        a[p, :8] = np.random.permutation(np.resize(levels, 8))
        for g in range(8):
            far = levels[np.abs(levels - a[p, g]) >= 10]
            a[p, g + 8] = far[np.random.randint(len(far))]
    return np.exp2(a.ravel()).repeat(32)


def f64(x):
    return np.asarray(x).astype(np.float64)


def striped8(idx):
    return np.concatenate([v.reshape(-1, 16).T for v in idx]).astype(np.uint16)


def unstriped8(offs):
    return np.stack([offs[16 * g:16 * g + 16].T.reshape(-1) for g in range(8)]).astype(np.int64)


K, N, T, J = 512, 512, 2048, 1024


def setup_inputs():
    n = np.random.standard_normal
    s = mx_kscale(K)[:, None]
    return {
        "xT": (n((K, T)) * s).astype(np.float32),
        "wgt": np.repeat(np.random.uniform(0.5, 2.0, (8, J)), 16, axis=0).astype(np.float32),
        "wk": (n((K, N)) / np.sqrt(K) / s).astype(np.float32),
        "wv": (n((K, N)) / np.sqrt(K) / s).astype(np.float32),
        "st": (n((N, J))).astype(np.float32),
        "offs": striped8(np.stack([np.random.permutation(T)[:J] for _ in range(8)])),
    }


def reference(xT, wgt, wk, wv, st, offs):
    idx = unstriped8(offs)
    rows = np.arange(K)
    xg = f64(wgt)[rows // 4 % 128] * f64(xT)[rows[:, None], idx[rows % 512 // 64]]
    xT_ = mxq(xg, 0, "e4m3")
    wk_ = mxq(f64(wk), 0, "e4m3")
    wv_ = mxq(f64(wv), 0, "e4m3")
    ke = wk_.T @ xT_
    ve = wv_.T @ xT_
    gate = np.tanh(ke * f64(st))
    return gate * ve

@@ -1,0 +1,144 @@
+from contextlib import ExitStack
+
+import concourse.mybir as mybir
+
+K, N, T, J = 512, 512, 2048, 1024
+FLOPS = 2 * 2 * K * N * J
+
+F32 = mybir.dt.float32
+BF16 = mybir.dt.bfloat16
+U32 = mybir.dt.uint32
+U16 = mybir.dt.uint16
+U8 = mybir.dt.uint8
+FP8X4 = mybir.dt.float8_e4m3fn_x4
+MULT = mybir.AluOpType.mult
+TANH = mybir.ActivationFunctionType.Tanh
+
+P = 128
+PACK = 4
+HALF = 512
+QUARTER = 256
+
+
+def tile_list_tanh_kernel(tc, xT, wgt, wk, wv, st, offs, out):
+    nc = tc.nc
+    with ExitStack() as ctx:
+        keep = ctx.enter_context(tc.tile_pool(name="keep", bufs=1))
+        psum = ctx.enter_context(tc.psum_pool(name="psum", bufs=4))
+
+        lists = keep.tile([P, J // 16], U16, name="lists")
+        wgt_sb = [keep.tile([P, HALF], F32, name="wgt%d" % h) for h in range(2)]
+        x_sb = [keep.tile([P, T], F32, name="x%d" % i) for i in range(PACK)]
+        wk_sb = keep.tile([P, PACK, N], F32, name="wk_sb")
+        wv_sb = keep.tile([P, PACK, N], F32, name="wv_sb")
+        st_sb = [keep.tile([P, J], F32, name="st%d" % t) for t in range(4)]
+        x_rows = xT.rearrange("(p i) t -> p i t", i=PACK)
+
+        nc.sync.dma_start(lists[:], offs)
+        nc.sync.dma_start(wgt_sb[0][:], wgt[:, 0:HALF])
+        nc.sync.dma_start(x_sb[0][:], x_rows[:, 0, :])
+        nc.sync.dma_start(wgt_sb[1][:], wgt[:, HALF:J])
+        for i in range(1, PACK):
+            nc.sync.dma_start(x_sb[i][:], x_rows[:, i, :])
+        nc.sync.dma_start(wk_sb[:], wk.rearrange("(p i) n -> p i n", i=PACK))
+        nc.sync.dma_start(st_sb[0][:, 0:HALF], st[0:P, 0:HALF])
+        nc.sync.dma_start(wv_sb[:], wv.rearrange("(p i) n -> p i n", i=PACK))
+        nc.sync.dma_start(st_sb[0][:, HALF:J], st[0:P, HALF:J])
+        for t in range(1, 4):
+            nc.sync.dma_start(st_sb[t][:], st[t * P:(t + 1) * P, :])
+
+        picked = [keep.tile([P, PACK, HALF], F32, name="picked%d" % h) for h in range(2)]
+        x_bf = [keep.tile([P, HALF, PACK], BF16, name="x_bf%d" % h, align_bytes=64) for h in range(2)]
+        x_codes = [keep.tile([P, HALF], U32, name="x_codes%d" % h, align_bytes=64) for h in range(2)]
+        x_scales = [keep.tile([P, HALF], U8, name="x_scales%d" % h, align_bytes=64) for h in range(2)]
+        w_raw = [wk_sb, wv_sb]
+        w_bf = [[keep.tile([P, P, PACK], BF16, name="w_bf%d_%d" % (s, t), align_bytes=64) for t in range(4)] for s in range(2)]
+        w_codes = [[keep.tile([P, P], U32, name="w_codes%d_%d" % (s, t), align_bytes=64) for t in range(4)] for s in range(2)]
+        w_scales = [[keep.tile([P, P], U8, name="w_scales%d_%d" % (s, t), align_bytes=64) for t in range(4)] for s in range(2)]
+
+        def gather(i, h, lo, hi):
+            j0 = h * HALF
+            nc.vector.tensor_tensor(
+                picked[h][:, i, lo:hi],
+                x_sb[i][:].indirect(lists[:, (j0 + lo) // 16:(j0 + hi) // 16]),
+                wgt_sb[h][:, lo:hi],
+                MULT,
+            )
+
+        def interleave(on_scalar, dst, src):
+            dst = dst.rearrange("p (c e) i -> p c i e", e=4)
+            src = src.rearrange("p i (c e) -> p c i e", e=4)
+            if on_scalar:
+                nc.scalar.copy(dst, src)
+            else:
+                nc.vector.tensor_copy(dst, src)
+
+        def quantize(codes, scales, grouped):
+            nc.vector.quantize_mx(
+                out=codes[:].bitcast(FP8X4), scales=scales[:], in_=grouped[:].rearrange("p c i -> p (c i)")
+            )
+
+        def round_w(s, t):
+            interleave(True, w_bf[s][t][:], w_raw[s][:, :, t * P:(t + 1) * P])
+
+        def quant_w(s, t):
+            quantize(w_codes[s][t], w_scales[s][t], w_bf[s][t])
+
+        def product(s, t, h):
+            acc = psum.tile([P, HALF], F32, name="acc%d" % s)
+            nc.tensor.matmul_mx(
+                out=acc[:],
+                lhsT=w_codes[s][t][:].bitcast(FP8X4),
+                lhsT_scale=w_scales[s][t][:],
+                rhs=x_codes[h][:].bitcast(FP8X4),
+                rhs_scale=x_scales[h][:],
+                start=True,
+                stop=True,
+            )
+            return acc
+
+        for i in range(PACK - 1):
+            for h in range(2):
+                gather(i, h, 0, HALF)
+        for h in range(2):
+            for lo in (0, QUARTER):
+                gather(PACK - 1, h, lo, lo + QUARTER)
+                if h == 0:
+                    interleave(True, x_bf[h][:, lo:lo + QUARTER, :], picked[h][:, :, lo:lo + QUARTER])
+        interleave(False, x_bf[1][:, 0:QUARTER, :], picked[1][:, :, 0:QUARTER])
+        quantize(x_codes[0], x_scales[0], x_bf[0])
+        interleave(False, x_bf[1][:, QUARTER:HALF, :], picked[1][:, :, QUARTER:HALF])
+        round_w(0, 0)
+        quant_w(0, 0)
+        quantize(x_codes[1], x_scales[1], x_bf[1])
+        round_w(0, 1)
+        quant_w(0, 1)
+        round_w(1, 0)
+        quant_w(1, 0)
+
+        gates = {}
+
+        def first(t, h):
+            ke = product(0, t, h)
+            z = keep.tile([P, HALF], F32, name="z%d_%d" % (t, h))
+            nc.vector.tensor_tensor(z[:], ke[:], st_sb[t][:, h * HALF:(h + 1) * HALF], MULT)
+            gate = keep.tile([P, HALF], F32, name="gate%d_%d" % (t, h))
+            nc.scalar.activation(gate[:], z[:], TANH)
+            gates[(t, h)] = gate
+
+        def second(t, h):
+            ve = product(1, t, h)
+            res = keep.tile([P, HALF], F32, name="res%d_%d" % (t, h))
+            nc.vector.tensor_tensor(res[:], ve[:], gates[(t, h)][:], MULT)
+            nc.sync.dma_start(out[t * P:(t + 1) * P, h * HALF:(h + 1) * HALF], res[:])
+
+        later = [(1, 1), (0, 2), (1, 2), (0, 3), (1, 3)]
+        tiles = [(t, h) for t in range(4) for h in range(2)]
+        for u in range(len(tiles) + 2):
+            if u < len(tiles):
+                first(*tiles[u])
+            if u < len(later):
+                round_w(*later[u])
+                quant_w(*later[u])
+            if u >= 2:
+                second(*tiles[u - 2])

@@ -12,133 +12,127 @@ U16 = mybir.dt.uint16
 U8 = mybir.dt.uint8
 FP8X4 = mybir.dt.float8_e4m3fn_x4
 MULT = mybir.AluOpType.mult
+ADD = mybir.AluOpType.add
 TANH = mybir.ActivationFunctionType.Tanh
 
 P = 128
 PACK = 4
 HALF = 512
-QUARTER = 256
+PLAN = [('ld', 'offs', 16384), ('ldw', 0, 512), ('ld', 'x0', 1048576), ('ldw', 512, 1024), ('ld', 'x1', 1048576), ('ld', 'x2', 1048576), ('ld', 'x3', 1048576), ('ld', 'wv', 1048576), ('ld', 'wk', 1048576), ('lds', 0, 0, 512), ('lds', 1, 0, 512), ('lds', 2, 0, 512), ('lds', 3, 0, 512), ('lds', 0, 512, 1024), ('lds', 1, 512, 1024), ('lds', 2, 512, 1024), ('lds', 3, 512, 1024), ('g', 0, 0, 512), ('g', 0, 512, 1024), ('g', 1, 0, 512), ('g', 1, 512, 1024), ('g', 2, 0, 512), ('g', 2, 512, 1024), ('g', 3, 0, 256), ('ilx', 'S', 0, 256), ('g', 3, 256, 512), ('g', 3, 512, 768), ('ilx', 'V', 256, 512), ('g', 3, 768, 1024), ('ilw', 'S', 1, 0, 2), ('ilw', 'S', 1, 2, 4), ('ilx', 'S', 512, 768), ('ilx', 'S', 768, 1024), ('qx', 0, 512), ('qw', 1, 0, 2), ('ilw', 'V', 0, 0, 2), ('qw', 1, 2, 4), ('qw', 0, 0, 2), ('ilw', 'V', 0, 2, 4), ('qx', 512, 768), ('qw', 0, 2, 4), ('qx', 768, 1024), ('m1', 0, 0, 512), ('m1', 1, 0, 512), ('m2', 'G', 0, 0, 512), ('m1', 2, 0, 512), ('m2', 'V', 1, 0, 512), ('m1', 3, 0, 512), ('m2', 'G', 2, 0, 512), ('m1', 0, 512, 1024), ('m2', 'V', 3, 0, 512), ('m1', 1, 512, 1024), ('m2', 'V', 0, 512, 1024), ('m1', 2, 512, 768), ('m1', 2, 768, 1024), ('m2', 'G', 1, 512, 768), ('m2', 'V', 1, 768, 1024), ('m1', 3, 512, 768), ('m1', 3, 768, 1024), ('m2', 'V', 2, 512, 768), ('m2', 'V', 2, 768, 1024), ('m2', 'V', 3, 512, 768), ('m2', 'V', 3, 768, 1024)]
 
 
 def tile_list_tanh_kernel(tc, xT, wgt, wk, wv, st, offs, out):
     nc = tc.nc
     with ExitStack() as ctx:
         keep = ctx.enter_context(tc.tile_pool(name="keep", bufs=1))
-        psum = ctx.enter_context(tc.psum_pool(name="psum", bufs=4))
+        psum_k = ctx.enter_context(tc.psum_pool(name="psum_k", bufs=4))
+        psum_v = ctx.enter_context(tc.psum_pool(name="psum_v", bufs=4))
 
         lists = keep.tile([P, J // 16], U16, name="lists")
-        wgt_sb = [keep.tile([P, HALF], F32, name="wgt%d" % h) for h in range(2)]
+        wgt_sb = keep.tile([P, J], F32, name="wgt_sb")
         x_sb = [keep.tile([P, T], F32, name="x%d" % i) for i in range(PACK)]
-        wk_sb = keep.tile([P, PACK, N], F32, name="wk_sb")
-        wv_sb = keep.tile([P, PACK, N], F32, name="wv_sb")
+        w_sb = [keep.tile([P, PACK, N], F32, name="w_sb%d" % s) for s in range(2)]
         st_sb = [keep.tile([P, J], F32, name="st%d" % t) for t in range(4)]
         x_rows = xT.rearrange("(p i) t -> p i t", i=PACK)
-
-        nc.sync.dma_start(lists[:], offs)
-        nc.sync.dma_start(wgt_sb[0][:], wgt[:, 0:HALF])
-        nc.sync.dma_start(x_sb[0][:], x_rows[:, 0, :])
-        nc.sync.dma_start(wgt_sb[1][:], wgt[:, HALF:J])
-        for i in range(1, PACK):
-            nc.sync.dma_start(x_sb[i][:], x_rows[:, i, :])
-        nc.sync.dma_start(wk_sb[:], wk.rearrange("(p i) n -> p i n", i=PACK))
-        nc.sync.dma_start(st_sb[0][:, 0:HALF], st[0:P, 0:HALF])
-        nc.sync.dma_start(wv_sb[:], wv.rearrange("(p i) n -> p i n", i=PACK))
-        nc.sync.dma_start(st_sb[0][:, HALF:J], st[0:P, HALF:J])
-        for t in range(1, 4):
-            nc.sync.dma_start(st_sb[t][:], st[t * P:(t + 1) * P, :])
-
+        w_rows = [w.rearrange("(p i) n -> p i n", i=PACK) for w in (wk, wv)]
         picked = [keep.tile([P, PACK, HALF], F32, name="picked%d" % h) for h in range(2)]
-        x_bf = [keep.tile([P, HALF, PACK], BF16, name="x_bf%d" % h, align_bytes=64) for h in range(2)]
-        x_codes = [keep.tile([P, HALF], U32, name="x_codes%d" % h, align_bytes=64) for h in range(2)]
-        x_scales = [keep.tile([P, HALF], U8, name="x_scales%d" % h, align_bytes=64) for h in range(2)]
-        w_raw = [wk_sb, wv_sb]
-        w_bf = [[keep.tile([P, P, PACK], BF16, name="w_bf%d_%d" % (s, t), align_bytes=64) for t in range(4)] for s in range(2)]
-        w_codes = [[keep.tile([P, P], U32, name="w_codes%d_%d" % (s, t), align_bytes=64) for t in range(4)] for s in range(2)]
-        w_scales = [[keep.tile([P, P], U8, name="w_scales%d_%d" % (s, t), align_bytes=64) for t in range(4)] for s in range(2)]
+        x_bf = keep.tile([P, J - 256, PACK], BF16, name="x_bf", align_bytes=64)
+        x_last = keep.tile([P, 256, PACK], BF16, name="x_last", tag="reused", align_bytes=64)
+        first_pool = []
+        x_codes = keep.tile([P, J], U32, name="x_codes", align_bytes=64)
+        x_scales = keep.tile([P, J], U8, name="x_scales", align_bytes=64)
+        w_bf = [keep.tile([P, N, PACK], BF16, name="w_bf%d" % s, align_bytes=64) for s in range(2)]
+        w_codes = [keep.tile([P, N], U32, name="w_codes%d" % s, align_bytes=64) for s in range(2)]
+        w_scales = [keep.tile([P, N], U8, name="w_scales%d" % s, align_bytes=64) for s in range(2)]
+        z = [keep.tile([P, J], F32, name="z%d" % t) for t in range(4)]
+        gate = [keep.tile([P, J], F32, name="gate%d" % t) for t in range(4)]
+        ve_sb = [keep.tile([P, J], F32, name="ve%d" % t) for t in range(4)]
+        res = [keep.tile([P, J], F32, name="res%d" % t) for t in range(4)]
 
-        def gather(i, h, lo, hi):
-            j0 = h * HALF
-            nc.vector.tensor_tensor(
-                picked[h][:, i, lo:hi],
-                x_sb[i][:].indirect(lists[:, (j0 + lo) // 16:(j0 + hi) // 16]),
-                wgt_sb[h][:, lo:hi],
-                MULT,
-            )
-
-        def interleave(on_scalar, dst, src):
+        def interleave(eng, dst, src):
             dst = dst.rearrange("p (c e) i -> p c i e", e=4)
             src = src.rearrange("p i (c e) -> p c i e", e=4)
-            if on_scalar:
+            if eng == "S":
                 nc.scalar.copy(dst, src)
-            else:
+            elif eng == "V":
                 nc.vector.tensor_copy(dst, src)
+            else:
+                nc.gpsimd.tensor_scalar(dst, src, 1.0, 0.0, MULT, ADD)
 
-        def quantize(codes, scales, grouped):
+        def quantize(codes, scales, grouped, lo, hi):
             nc.vector.quantize_mx(
-                out=codes[:].bitcast(FP8X4), scales=scales[:], in_=grouped[:].rearrange("p c i -> p (c i)")
+                out=codes[:, lo:hi].bitcast(FP8X4),
+                scales=scales[:, lo:hi],
+                in_=grouped.rearrange("p c i -> p (c i)"),
             )
 
-        def round_w(s, t):
-            interleave(True, w_bf[s][t][:], w_raw[s][:, :, t * P:(t + 1) * P])
-
-        def quant_w(s, t):
-            quantize(w_codes[s][t], w_scales[s][t], w_bf[s][t])
-
-        def product(s, t, h):
-            acc = psum.tile([P, HALF], F32, name="acc%d" % s)
+        def product(s, t, lo, hi):
+            pool = psum_k if s == 0 else psum_v
+            acc = pool.tile([P, HALF], F32, name="acc%d" % s)
             nc.tensor.matmul_mx(
-                out=acc[:],
-                lhsT=w_codes[s][t][:].bitcast(FP8X4),
-                lhsT_scale=w_scales[s][t][:],
-                rhs=x_codes[h][:].bitcast(FP8X4),
-                rhs_scale=x_scales[h][:],
+                out=acc[:, 0:hi - lo],
+                lhsT=w_codes[s][:, t * P:(t + 1) * P].bitcast(FP8X4),
+                lhsT_scale=w_scales[s][:, t * P:(t + 1) * P],
+                rhs=x_codes[:, lo:hi].bitcast(FP8X4),
+                rhs_scale=x_scales[:, lo:hi],
                 start=True,
                 stop=True,
             )
-            return acc
+            return acc[:, 0:hi - lo]
 
-        for i in range(PACK - 1):
-            for h in range(2):
-                gather(i, h, 0, HALF)
-        for h in range(2):
-            for lo in (0, QUARTER):
-                gather(PACK - 1, h, lo, lo + QUARTER)
-                if h == 0:
-                    interleave(True, x_bf[h][:, lo:lo + QUARTER, :], picked[h][:, :, lo:lo + QUARTER])
-        interleave(False, x_bf[1][:, 0:QUARTER, :], picked[1][:, :, 0:QUARTER])
-        quantize(x_codes[0], x_scales[0], x_bf[0])
-        interleave(False, x_bf[1][:, QUARTER:HALF, :], picked[1][:, :, QUARTER:HALF])
-        round_w(0, 0)
-        quant_w(0, 0)
-        quantize(x_codes[1], x_scales[1], x_bf[1])
-        round_w(0, 1)
-        quant_w(0, 1)
-        round_w(1, 0)
-        quant_w(1, 0)
-
-        gates = {}
-
-        def first(t, h):
-            ke = product(0, t, h)
-            z = keep.tile([P, HALF], F32, name="z%d_%d" % (t, h))
-            nc.vector.tensor_tensor(z[:], ke[:], st_sb[t][:, h * HALF:(h + 1) * HALF], MULT)
-            gate = keep.tile([P, HALF], F32, name="gate%d_%d" % (t, h))
-            nc.scalar.activation(gate[:], z[:], TANH)
-            gates[(t, h)] = gate
-
-        def second(t, h):
-            ve = product(1, t, h)
-            res = keep.tile([P, HALF], F32, name="res%d_%d" % (t, h))
-            nc.vector.tensor_tensor(res[:], ve[:], gates[(t, h)][:], MULT)
-            nc.sync.dma_start(out[t * P:(t + 1) * P, h * HALF:(h + 1) * HALF], res[:])
-
-        later = [(1, 1), (0, 2), (1, 2), (0, 3), (1, 3)]
-        tiles = [(t, h) for t in range(4) for h in range(2)]
-        for u in range(len(tiles) + 2):
-            if u < len(tiles):
-                first(*tiles[u])
-            if u < len(later):
-                round_w(*later[u])
-                quant_w(*later[u])
-            if u >= 2:
-                second(*tiles[u - 2])
+        for op in PLAN:
+            kind = op[0]
+            if kind == "ld":
+                if op[1] == "offs":
+                    nc.sync.dma_start(lists[:], offs)
+                elif op[1] in ("wk", "wv"):
+                    s = 0 if op[1] == "wk" else 1
+                    nc.sync.dma_start(w_sb[s][:], w_rows[s])
+                else:
+                    i = int(op[1][1])
+                    nc.sync.dma_start(x_sb[i][:], x_rows[:, i, :])
+            elif kind == "ldw":
+                nc.sync.dma_start(wgt_sb[:, op[1]:op[2]], wgt[:, op[1]:op[2]])
+            elif kind == "lds":
+                t, lo, hi = op[1:]
+                nc.sync.dma_start(st_sb[t][:, lo:hi], st[t * P:(t + 1) * P, lo:hi])
+            elif kind == "g":
+                i, lo, hi = op[1:]
+                h = lo // HALF
+                nc.vector.tensor_tensor(
+                    picked[h][:, i, lo - h * HALF:hi - h * HALF],
+                    x_sb[i][:].indirect(lists[:, lo // 16:hi // 16]),
+                    wgt_sb[:, lo:hi],
+                    MULT,
+                )
+            elif kind == "ilx":
+                eng, lo, hi = op[1:]
+                h = lo // HALF
+                interleave(eng, x_bf[:, lo:hi, :] if lo < 768 else x_last[:], picked[h][:, :, lo - h * HALF:hi - h * HALF])
+            elif kind == "qx":
+                quantize(x_codes, x_scales, x_bf[:, op[1]:op[2], :] if op[1] < 768 else x_last[:], op[1], op[2])
+            elif kind == "ilw":
+                eng, s, a, b = op[1:]
+                interleave(eng, w_bf[s][:, a * P:b * P, :], w_sb[s][:, :, a * P:b * P])
+            elif kind == "qw":
+                s, a, b = op[1:]
+                quantize(w_codes[s], w_scales[s], w_bf[s][:, a * P:b * P, :], a * P, b * P)
+            elif kind == "m1":
+                t, lo, hi = op[1:]
+                ke = product(0, t, lo, hi)
+                nc.vector.tensor_tensor(z[t][:, lo:hi], ke, st_sb[t][:, lo:hi], MULT)
+                nc.scalar.activation(gate[t][:, lo:hi], z[t][:, lo:hi], TANH)
+            else:
+                eng, t, lo, hi = op[1:]
+                ve = product(1, t, lo, hi)
+                dst = res[t][:, lo:hi]
+                if eng == "G" and not first_pool:
+                    held = keep.tile([P, HALF], F32, name="held", tag="reused", align_bytes=64)
+                    first_pool.append(held)
+                    dst = held[:, 0:hi - lo]
+                if eng == "V":
+                    nc.vector.tensor_tensor(dst, ve, gate[t][:, lo:hi], MULT)
+                else:
+                    nc.scalar.copy(ve_sb[t][:, lo:hi], ve)
+                    nc.gpsimd.tensor_tensor(dst, ve_sb[t][:, lo:hi], gate[t][:, lo:hi], MULT)
+                nc.sync.dma_start(out[t * P:(t + 1) * P, lo:hi], dst)

@@ -18,7 +18,7 @@ TANH = mybir.ActivationFunctionType.Tanh
 P = 128
 PACK = 4
 HALF = 512
-PLAN = [('ld', 'offs', 16384), ('ldw', 0, 512), ('ld', 'x0', 1048576), ('ldw', 512, 1024), ('ld', 'x1', 1048576), ('ld', 'x2', 1048576), ('ld', 'x3', 1048576), ('ld', 'wv', 1048576), ('ld', 'wk', 1048576), ('lds', 0, 0, 512), ('lds', 1, 0, 512), ('lds', 2, 0, 512), ('lds', 3, 0, 512), ('lds', 0, 512, 1024), ('lds', 1, 512, 1024), ('lds', 2, 512, 1024), ('lds', 3, 512, 1024), ('g', 0, 0, 512), ('g', 0, 512, 1024), ('g', 1, 0, 512), ('g', 1, 512, 1024), ('g', 2, 0, 512), ('g', 2, 512, 1024), ('g', 3, 0, 256), ('ilx', 'S', 0, 256), ('g', 3, 256, 512), ('g', 3, 512, 768), ('ilx', 'V', 256, 512), ('g', 3, 768, 1024), ('ilw', 'S', 1, 0, 2), ('ilw', 'S', 1, 2, 4), ('ilx', 'S', 512, 768), ('ilx', 'S', 768, 1024), ('qx', 0, 512), ('qw', 1, 0, 2), ('ilw', 'V', 0, 0, 2), ('qw', 1, 2, 4), ('qw', 0, 0, 2), ('ilw', 'V', 0, 2, 4), ('qx', 512, 768), ('qw', 0, 2, 4), ('qx', 768, 1024), ('m1', 0, 0, 512), ('m1', 1, 0, 512), ('m2', 'G', 0, 0, 512), ('m1', 2, 0, 512), ('m2', 'V', 1, 0, 512), ('m1', 3, 0, 512), ('m2', 'G', 2, 0, 512), ('m1', 0, 512, 1024), ('m2', 'V', 3, 0, 512), ('m1', 1, 512, 1024), ('m2', 'V', 0, 512, 1024), ('m1', 2, 512, 768), ('m1', 2, 768, 1024), ('m2', 'G', 1, 512, 768), ('m2', 'V', 1, 768, 1024), ('m1', 3, 512, 768), ('m1', 3, 768, 1024), ('m2', 'V', 2, 512, 768), ('m2', 'V', 2, 768, 1024), ('m2', 'V', 3, 512, 768), ('m2', 'V', 3, 768, 1024)]
+PLAN = [('ldz',), ('ld', 'x0', 1048576), ('ld', 'offs', 16384), ('ld', 'x1', 1048576), ('ld', 'x2', 1048576), ('ld', 'x3', 1048576), ('ld', 'wk', 1048576), ('ld', 'wv', 1048576), ('lds', 0, 0, 512), ('lds', 1, 0, 512), ('lds', 2, 0, 512), ('lds', 3, 0, 512), ('lds', 0, 512, 1024), ('lds', 1, 512, 1024), ('lds', 2, 512, 1024), ('lds', 3, 512, 1024), ('spread',), ('g', 0, 0, 512), ('g', 0, 512, 1024), ('g', 1, 0, 512), ('g', 1, 512, 1024), ('g', 2, 0, 512), ('g', 2, 512, 1024), ('g', 3, 0, 256), ('ilx', 'S', 0, 256), ('g', 3, 256, 512), ('g', 3, 512, 768), ('ilx', 'V', 256, 512), ('ilx', 'S', 512, 768), ('g', 3, 768, 1024), ('ilw', 'S', 0, 2, 4), ('ilw', 'S', 1, 0, 2), ('ilx', 'S', 768, 1024), ('qx', 0, 512), ('ilw', 'V', 0, 0, 2), ('qx', 512, 768), ('qw', 0, 0, 2), ('ilw', 'V', 1, 2, 4), ('qw', 0, 2, 4), ('m1', 0, 0, 512), ('qw', 1, 2, 4), ('qx', 768, 1024), ('qw', 1, 0, 2), ('m1', 1, 0, 512), ('m2', 'G', 0, 0, 512), ('m1', 2, 0, 512), ('m2', 'V', 1, 0, 512), ('m1', 3, 0, 512), ('m2', 'G', 2, 0, 256), ('m2', 'V', 2, 256, 512), ('m1', 0, 512, 1024), ('m2', 'G', 3, 0, 256), ('m2', 'V', 3, 256, 512), ('m1', 1, 512, 1024), ('m2', 'V', 0, 512, 1024), ('m1', 2, 512, 768), ('m1', 2, 768, 1024), ('m2', 'G', 1, 512, 768), ('m2', 'V', 1, 768, 1024), ('m1', 3, 512, 768), ('m1', 3, 768, 1024), ('m2', 'V', 2, 512, 768), ('m2', 'V', 2, 768, 1024), ('m2', 'V', 3, 512, 768), ('m2', 'V', 3, 768, 1024)]
 
 
 def tile_list_tanh_kernel(tc, xT, wgt, wk, wv, st, offs, out):
@@ -29,7 +29,10 @@ def tile_list_tanh_kernel(tc, xT, wgt, wk, wv, st, offs, out):
         psum_v = ctx.enter_context(tc.psum_pool(name="psum_v", bufs=4))
 
         lists = keep.tile([P, J // 16], U16, name="lists")
-        wgt_sb = keep.tile([P, J], F32, name="wgt_sb")
+        wgt_sb = keep.tile([P, J], F32, name="wgt_sb", align_bytes=64)
+        w_in = keep.tile([P, 64], F32, name="w_in", align_bytes=64)
+        w_turned = keep.tile([P, 64], F32, name="w_turned", align_bytes=64)
+        w_spread = keep.tile([P, J], F32, name="w_spread", align_bytes=64)
         x_sb = [keep.tile([P, T], F32, name="x%d" % i) for i in range(PACK)]
         w_sb = [keep.tile([P, PACK, N], F32, name="w_sb%d" % s) for s in range(2)]
         st_sb = [keep.tile([P, J], F32, name="st%d" % t) for t in range(4)]
@@ -93,6 +96,21 @@ def tile_list_tanh_kernel(tc, xT, wgt, wk, wv, st, offs, out):
                     nc.sync.dma_start(x_sb[i][:], x_rows[:, i, :])
             elif kind == "ldw":
                 nc.sync.dma_start(wgt_sb[:, op[1]:op[2]], wgt[:, op[1]:op[2]])
+            elif kind == "ldz":
+                nc.sync.dma_start(w_in[:], wgt.rearrange("(g r) (m c) -> g r m c", r=16, c=64)[:, 0, :, :])
+            elif kind == "spread":
+                for e in range(2):
+                    nc.vector.transpose(w_turned[:, 32 * e:32 * e + 32], w_in[:, 32 * e:32 * e + 32])
+                for h in range(2):
+                    src = w_turned[:].rearrange("p (q m) -> p m q", m=16)[:, 8 * h:8 * h + 8, :]
+                    src = src.unsqueeze(3).to_broadcast([P, 8, 4, 16])
+                    dst = w_spread[:, h * HALF:(h + 1) * HALF].rearrange("p (m q r) -> p m q r", q=4, r=16)
+                    if h == 0:
+                        nc.vector.tensor_copy(dst, src)
+                    else:
+                        nc.scalar.copy(dst, src)
+                for h in range(2):
+                    nc.vector.transpose(wgt_sb[:, h * HALF:(h + 1) * HALF], w_spread[:, h * HALF:(h + 1) * HALF])
             elif kind == "lds":
                 t, lo, hi = op[1:]
                 nc.sync.dma_start(st_sb[t][:, lo:hi], st[t * P:(t + 1) * P, lo:hi])

@@ -18,7 +18,7 @@ TANH = mybir.ActivationFunctionType.Tanh
 P = 128
 PACK = 4
 HALF = 512
-PLAN = [('ldz',), ('ld', 'x0', 1048576), ('ld', 'offs', 16384), ('ld', 'x1', 1048576), ('ld', 'x2', 1048576), ('ld', 'x3', 1048576), ('ld', 'wk', 1048576), ('ld', 'wv', 1048576), ('lds', 0, 0, 512), ('lds', 1, 0, 512), ('lds', 2, 0, 512), ('lds', 3, 0, 512), ('lds', 0, 512, 1024), ('lds', 1, 512, 1024), ('lds', 2, 512, 1024), ('lds', 3, 512, 1024), ('spread',), ('g', 0, 0, 512), ('g', 0, 512, 1024), ('g', 1, 0, 512), ('g', 1, 512, 1024), ('g', 2, 0, 512), ('g', 2, 512, 1024), ('g', 3, 0, 256), ('ilx', 'S', 0, 256), ('g', 3, 256, 512), ('g', 3, 512, 768), ('ilx', 'V', 256, 512), ('ilx', 'S', 512, 768), ('g', 3, 768, 1024), ('ilw', 'S', 0, 2, 4), ('ilw', 'S', 1, 0, 2), ('ilx', 'S', 768, 1024), ('qx', 0, 512), ('ilw', 'V', 0, 0, 2), ('qx', 512, 768), ('qw', 0, 0, 2), ('ilw', 'V', 1, 2, 4), ('qw', 0, 2, 4), ('m1', 0, 0, 512), ('qw', 1, 2, 4), ('qx', 768, 1024), ('qw', 1, 0, 2), ('m1', 1, 0, 512), ('m2', 'G', 0, 0, 512), ('m1', 2, 0, 512), ('m2', 'V', 1, 0, 512), ('m1', 3, 0, 512), ('m2', 'G', 2, 0, 256), ('m2', 'V', 2, 256, 512), ('m1', 0, 512, 1024), ('m2', 'G', 3, 0, 256), ('m2', 'V', 3, 256, 512), ('m1', 1, 512, 1024), ('m2', 'V', 0, 512, 1024), ('m1', 2, 512, 768), ('m1', 2, 768, 1024), ('m2', 'G', 1, 512, 768), ('m2', 'V', 1, 768, 1024), ('m1', 3, 512, 768), ('m1', 3, 768, 1024), ('m2', 'V', 2, 512, 768), ('m2', 'V', 2, 768, 1024), ('m2', 'V', 3, 512, 768), ('m2', 'V', 3, 768, 1024)]
+PLAN = [('ld', 'offs', 16384), ('ldw', 0, 512), ('ld', 'x0', 1048576), ('ldw', 512, 1024), ('ld', 'x1', 1048576), ('ld', 'x2', 1048576), ('ld', 'x3', 1048576), ('ld', 'wk', 1048576), ('ld', 'wv', 1048576), ('lds', 0, 0, 512), ('lds', 1, 0, 512), ('lds', 2, 0, 512), ('lds', 3, 0, 512), ('lds', 0, 512, 1024), ('lds', 1, 512, 1024), ('lds', 2, 512, 1024), ('lds', 3, 512, 1024), ('g', 0, 0, 512), ('g', 0, 512, 1024), ('g', 1, 0, 512), ('g', 1, 512, 1024), ('g', 2, 0, 512), ('g', 2, 512, 1024), ('g', 3, 0, 256), ('ilx', 'S', 0, 256), ('g', 3, 256, 512), ('g', 3, 512, 768), ('ilx', 'V', 256, 512), ('ilx', 'S', 512, 768), ('g', 3, 768, 1024), ('ilw', 'S', 0, 2, 4), ('ilw', 'S', 1, 0, 2), ('ilx', 'S', 768, 1024), ('qx', 0, 512), ('ilw', 'V', 0, 0, 2), ('qx', 512, 768), ('qw', 0, 0, 2), ('ilw', 'V', 1, 2, 4), ('qw', 0, 2, 4), ('m1', 0, 0, 512), ('qw', 1, 2, 4), ('qx', 768, 1024), ('qw', 1, 0, 2), ('m1', 1, 0, 512), ('m2', 'G', 0, 0, 512), ('m1', 2, 0, 512), ('m2', 'V', 1, 0, 512), ('m1', 3, 0, 512), ('m2', 'G', 2, 0, 256), ('m2', 'V', 2, 256, 512), ('m1', 0, 512, 1024), ('m2', 'G', 3, 0, 256), ('m2', 'V', 3, 256, 512), ('m1', 1, 512, 1024), ('m2', 'V', 0, 512, 1024), ('m1', 2, 512, 768), ('m1', 2, 768, 1024), ('m2', 'G', 1, 512, 768), ('m2', 'V', 1, 768, 1024), ('m1', 3, 512, 768), ('m1', 3, 768, 1024), ('m2', 'V', 2, 512, 768), ('m2', 'V', 2, 768, 1024), ('m2', 'V', 3, 512, 768), ('m2', 'V', 3, 768, 1024)]
 
 
 def tile_list_tanh_kernel(tc, xT, wgt, wk, wv, st, offs, out):
@@ -29,10 +29,7 @@ def tile_list_tanh_kernel(tc, xT, wgt, wk, wv, st, offs, out):
         psum_v = ctx.enter_context(tc.psum_pool(name="psum_v", bufs=4))
 
         lists = keep.tile([P, J // 16], U16, name="lists")
-        wgt_sb = keep.tile([P, J], F32, name="wgt_sb", align_bytes=64)
-        w_in = keep.tile([P, 64], F32, name="w_in", align_bytes=64)
-        w_turned = keep.tile([P, 64], F32, name="w_turned", align_bytes=64)
-        w_spread = keep.tile([P, J], F32, name="w_spread", align_bytes=64)
+        wgt_sb = keep.tile([P, J], F32, name="wgt_sb")
         x_sb = [keep.tile([P, T], F32, name="x%d" % i) for i in range(PACK)]
         w_sb = [keep.tile([P, PACK, N], F32, name="w_sb%d" % s) for s in range(2)]
         st_sb = [keep.tile([P, J], F32, name="st%d" % t) for t in range(4)]
@@ -96,21 +93,6 @@ def tile_list_tanh_kernel(tc, xT, wgt, wk, wv, st, offs, out):
                     nc.sync.dma_start(x_sb[i][:], x_rows[:, i, :])
             elif kind == "ldw":
                 nc.sync.dma_start(wgt_sb[:, op[1]:op[2]], wgt[:, op[1]:op[2]])
-            elif kind == "ldz":
-                nc.sync.dma_start(w_in[:], wgt.rearrange("(g r) (m c) -> g r m c", r=16, c=64)[:, 0, :, :])
-            elif kind == "spread":
-                for e in range(2):
-                    nc.vector.transpose(w_turned[:, 32 * e:32 * e + 32], w_in[:, 32 * e:32 * e + 32])
-                for h in range(2):
-                    src = w_turned[:].rearrange("p (q m) -> p m q", m=16)[:, 8 * h:8 * h + 8, :]
-                    src = src.unsqueeze(3).to_broadcast([P, 8, 4, 16])
-                    dst = w_spread[:, h * HALF:(h + 1) * HALF].rearrange("p (m q r) -> p m q r", q=4, r=16)
-                    if h == 0:
-                        nc.vector.tensor_copy(dst, src)
-                    else:
-                        nc.scalar.copy(dst, src)
-                for h in range(2):
-                    nc.vector.transpose(wgt_sb[:, h * HALF:(h + 1) * HALF], w_spread[:, h * HALF:(h + 1) * HALF])
             elif kind == "lds":
                 t, lo, hi = op[1:]
                 nc.sync.dma_start(st_sb[t][:, lo:hi], st[t * P:(t + 1) * P, lo:hi])

@@ -12,62 +12,84 @@ U16 = mybir.dt.uint16
 U8 = mybir.dt.uint8
 FP8X4 = mybir.dt.float8_e4m3fn_x4
 MULT = mybir.AluOpType.mult
-ADD = mybir.AluOpType.add
 TANH = mybir.ActivationFunctionType.Tanh
 
 P = 128
 PACK = 4
-HALF = 512
-PLAN = [('ld', 'offs', 16384), ('ldw', 0, 512), ('ld', 'x0', 1048576), ('ldw', 512, 1024), ('ld', 'x1', 1048576), ('ld', 'x2', 1048576), ('ld', 'x3', 1048576), ('ld', 'wk', 1048576), ('ld', 'wv', 1048576), ('lds', 0, 0, 512), ('lds', 1, 0, 512), ('lds', 2, 0, 512), ('lds', 3, 0, 512), ('lds', 0, 512, 1024), ('lds', 1, 512, 1024), ('lds', 2, 512, 1024), ('lds', 3, 512, 1024), ('g', 0, 0, 512), ('g', 0, 512, 1024), ('g', 1, 0, 512), ('g', 1, 512, 1024), ('g', 2, 0, 512), ('g', 2, 512, 1024), ('g', 3, 0, 256), ('ilx', 'S', 0, 256), ('g', 3, 256, 512), ('g', 3, 512, 768), ('ilx', 'V', 256, 512), ('ilx', 'S', 512, 768), ('g', 3, 768, 1024), ('ilw', 'S', 0, 2, 4), ('ilw', 'S', 1, 0, 2), ('ilx', 'S', 768, 1024), ('qx', 0, 512), ('ilw', 'V', 0, 0, 2), ('qx', 512, 768), ('qw', 0, 0, 2), ('ilw', 'V', 1, 2, 4), ('qw', 0, 2, 4), ('m1', 0, 0, 512), ('qw', 1, 2, 4), ('qx', 768, 1024), ('qw', 1, 0, 2), ('m1', 1, 0, 512), ('m2', 'G', 0, 0, 512), ('m1', 2, 0, 512), ('m2', 'V', 1, 0, 512), ('m1', 3, 0, 512), ('m2', 'G', 2, 0, 256), ('m2', 'V', 2, 256, 512), ('m1', 0, 512, 1024), ('m2', 'G', 3, 0, 256), ('m2', 'V', 3, 256, 512), ('m1', 1, 512, 1024), ('m2', 'V', 0, 512, 1024), ('m1', 2, 512, 768), ('m1', 2, 768, 1024), ('m2', 'G', 1, 512, 768), ('m2', 'V', 1, 768, 1024), ('m1', 3, 512, 768), ('m1', 3, 768, 1024), ('m2', 'V', 2, 512, 768), ('m2', 'V', 2, 768, 1024), ('m2', 'V', 3, 512, 768), ('m2', 'V', 3, 768, 1024)]
+LIST_GROUP = 16
+HALF = J // 2
+QUARTER = J // 4
+LAST_QUARTER = J - QUARTER
+ROW_BLOCKS = N // P
+KEY, VALUE = 0, 1
+BANKS_EACH = 4
+
+PIECES = [(t, h * HALF) for h in range(2) for t in range(ROW_BLOCKS)]
+GPSIMD_COLUMNS = {0: HALF, 2: QUARTER, 3: QUARTER, 5: QUARTER}
+FIRST_SPLIT_PIECE = len(PIECES) - 2
 
 
 def tile_list_tanh_kernel(tc, xT, wgt, wk, wv, st, offs, out):
     nc = tc.nc
     with ExitStack() as ctx:
         keep = ctx.enter_context(tc.tile_pool(name="keep", bufs=1))
-        psum_k = ctx.enter_context(tc.psum_pool(name="psum_k", bufs=4))
-        psum_v = ctx.enter_context(tc.psum_pool(name="psum_v", bufs=4))
+        psum_k = ctx.enter_context(tc.psum_pool(name="psum_k", bufs=BANKS_EACH))
+        psum_v = ctx.enter_context(tc.psum_pool(name="psum_v", bufs=BANKS_EACH))
 
-        lists = keep.tile([P, J // 16], U16, name="lists")
+        lists = keep.tile([P, J // LIST_GROUP], U16, name="lists")
         wgt_sb = keep.tile([P, J], F32, name="wgt_sb")
         x_sb = [keep.tile([P, T], F32, name="x%d" % i) for i in range(PACK)]
-        w_sb = [keep.tile([P, PACK, N], F32, name="w_sb%d" % s) for s in range(2)]
-        st_sb = [keep.tile([P, J], F32, name="st%d" % t) for t in range(4)]
-        x_rows = xT.rearrange("(p i) t -> p i t", i=PACK)
-        w_rows = [w.rearrange("(p i) n -> p i n", i=PACK) for w in (wk, wv)]
+        w_sb = [keep.tile([P, PACK, N], F32, name="w_sb%d" % s) for s in (KEY, VALUE)]
+        st_sb = [keep.tile([P, J], F32, name="st%d" % t) for t in range(ROW_BLOCKS)]
         picked = [keep.tile([P, PACK, HALF], F32, name="picked%d" % h) for h in range(2)]
-        x_bf = keep.tile([P, J - 256, PACK], BF16, name="x_bf", align_bytes=64)
-        x_last = keep.tile([P, 256, PACK], BF16, name="x_last", tag="reused", align_bytes=64)
-        first_pool = []
+        x_bf = keep.tile([P, LAST_QUARTER, PACK], BF16, name="x_bf", align_bytes=64)
+        x_last = keep.tile([P, QUARTER, PACK], BF16, name="x_last", tag="reused", align_bytes=64)
         x_codes = keep.tile([P, J], U32, name="x_codes", align_bytes=64)
         x_scales = keep.tile([P, J], U8, name="x_scales", align_bytes=64)
-        w_bf = [keep.tile([P, N, PACK], BF16, name="w_bf%d" % s, align_bytes=64) for s in range(2)]
-        w_codes = [keep.tile([P, N], U32, name="w_codes%d" % s, align_bytes=64) for s in range(2)]
-        w_scales = [keep.tile([P, N], U8, name="w_scales%d" % s, align_bytes=64) for s in range(2)]
-        z = [keep.tile([P, J], F32, name="z%d" % t) for t in range(4)]
-        gate = [keep.tile([P, J], F32, name="gate%d" % t) for t in range(4)]
-        ve_sb = [keep.tile([P, J], F32, name="ve%d" % t) for t in range(4)]
-        res = [keep.tile([P, J], F32, name="res%d" % t) for t in range(4)]
+        w_bf = [keep.tile([P, N, PACK], BF16, name="w_bf%d" % s, align_bytes=64) for s in (KEY, VALUE)]
+        w_codes = [keep.tile([P, N], U32, name="w_codes%d" % s, align_bytes=64) for s in (KEY, VALUE)]
+        w_scales = [keep.tile([P, N], U8, name="w_scales%d" % s, align_bytes=64) for s in (KEY, VALUE)]
+        z = [keep.tile([P, J], F32, name="z%d" % t) for t in range(ROW_BLOCKS)]
+        gate = [keep.tile([P, J], F32, name="gate%d" % t) for t in range(ROW_BLOCKS)]
+        ve_sb = [keep.tile([P, J], F32, name="ve%d" % t) for t in range(ROW_BLOCKS)]
+        res = [keep.tile([P, J], F32, name="res%d" % t) for t in range(ROW_BLOCKS)]
 
-        def interleave(eng, dst, src):
-            dst = dst.rearrange("p (c e) i -> p c i e", e=4)
-            src = src.rearrange("p i (c e) -> p c i e", e=4)
-            if eng == "S":
-                nc.scalar.copy(dst, src)
-            elif eng == "V":
-                nc.vector.tensor_copy(dst, src)
-            else:
-                nc.gpsimd.tensor_scalar(dst, src, 1.0, 0.0, MULT, ADD)
-
-        def quantize(codes, scales, grouped, lo, hi):
-            nc.vector.quantize_mx(
-                out=codes[:, lo:hi].bitcast(FP8X4),
-                scales=scales[:, lo:hi],
-                in_=grouped.rearrange("p c i -> p (c i)"),
+        def gather(i, lo, hi):
+            h, at = divmod(lo, HALF)
+            nc.vector.tensor_tensor(
+                picked[h][:, i, at:at + hi - lo],
+                x_sb[i][:].indirect(lists[:, lo // LIST_GROUP:hi // LIST_GROUP]),
+                wgt_sb[:, lo:hi],
+                MULT,
             )
 
+        def round_and_interleave(copy, dst, src):
+            copy(dst.rearrange("p (c e) i -> p c i e", e=4), src.rearrange("p i (c e) -> p c i e", e=4))
+
+        def x_grouped(lo, hi):
+            return x_last[:] if lo == LAST_QUARTER else x_bf[:, lo:hi, :]
+
+        def round_x(copy, quarter):
+            lo = quarter * QUARTER
+            h, at = divmod(lo, HALF)
+            round_and_interleave(copy, x_grouped(lo, lo + QUARTER), picked[h][:, :, at:at + QUARTER])
+
+        def round_w(copy, s, lo, hi):
+            round_and_interleave(copy, w_bf[s][:, lo:hi, :], w_sb[s][:, :, lo:hi])
+
+        def quantize(codes, scales, grouped):
+            nc.vector.quantize_mx(
+                out=codes.bitcast(FP8X4), scales=scales, in_=grouped.rearrange("p c i -> p (c i)")
+            )
+
+        def quantize_x(lo, hi):
+            quantize(x_codes[:, lo:hi], x_scales[:, lo:hi], x_grouped(lo, hi))
+
+        def quantize_w(s, lo, hi):
+            quantize(w_codes[s][:, lo:hi], w_scales[s][:, lo:hi], w_bf[s][:, lo:hi, :])
+
         def product(s, t, lo, hi):
-            pool = psum_k if s == 0 else psum_v
+            pool = psum_k if s == KEY else psum_v
             acc = pool.tile([P, HALF], F32, name="acc%d" % s)
             nc.tensor.matmul_mx(
                 out=acc[:, 0:hi - lo],
@@ -80,59 +102,81 @@ def tile_list_tanh_kernel(tc, xT, wgt, wk, wv, st, offs, out):
             )
             return acc[:, 0:hi - lo]
 
-        for op in PLAN:
-            kind = op[0]
-            if kind == "ld":
-                if op[1] == "offs":
-                    nc.sync.dma_start(lists[:], offs)
-                elif op[1] in ("wk", "wv"):
-                    s = 0 if op[1] == "wk" else 1
-                    nc.sync.dma_start(w_sb[s][:], w_rows[s])
-                else:
-                    i = int(op[1][1])
-                    nc.sync.dma_start(x_sb[i][:], x_rows[:, i, :])
-            elif kind == "ldw":
-                nc.sync.dma_start(wgt_sb[:, op[1]:op[2]], wgt[:, op[1]:op[2]])
-            elif kind == "lds":
-                t, lo, hi = op[1:]
-                nc.sync.dma_start(st_sb[t][:, lo:hi], st[t * P:(t + 1) * P, lo:hi])
-            elif kind == "g":
-                i, lo, hi = op[1:]
-                h = lo // HALF
-                nc.vector.tensor_tensor(
-                    picked[h][:, i, lo - h * HALF:hi - h * HALF],
-                    x_sb[i][:].indirect(lists[:, lo // 16:hi // 16]),
-                    wgt_sb[:, lo:hi],
-                    MULT,
-                )
-            elif kind == "ilx":
-                eng, lo, hi = op[1:]
-                h = lo // HALF
-                interleave(eng, x_bf[:, lo:hi, :] if lo < 768 else x_last[:], picked[h][:, :, lo - h * HALF:hi - h * HALF])
-            elif kind == "qx":
-                quantize(x_codes, x_scales, x_bf[:, op[1]:op[2], :] if op[1] < 768 else x_last[:], op[1], op[2])
-            elif kind == "ilw":
-                eng, s, a, b = op[1:]
-                interleave(eng, w_bf[s][:, a * P:b * P, :], w_sb[s][:, :, a * P:b * P])
-            elif kind == "qw":
-                s, a, b = op[1:]
-                quantize(w_codes[s], w_scales[s], w_bf[s][:, a * P:b * P, :], a * P, b * P)
-            elif kind == "m1":
-                t, lo, hi = op[1:]
-                ke = product(0, t, lo, hi)
-                nc.vector.tensor_tensor(z[t][:, lo:hi], ke, st_sb[t][:, lo:hi], MULT)
-                nc.scalar.activation(gate[t][:, lo:hi], z[t][:, lo:hi], TANH)
+        def make_gate(t, lo, hi):
+            ke = product(KEY, t, lo, hi)
+            nc.vector.tensor_tensor(z[t][:, lo:hi], ke, st_sb[t][:, lo:hi], MULT)
+            nc.scalar.activation(gate[t][:, lo:hi], z[t][:, lo:hi], TANH)
+
+        def finish_on_vector(t, lo, hi):
+            ve = product(VALUE, t, lo, hi)
+            nc.vector.tensor_tensor(res[t][:, lo:hi], ve, gate[t][:, lo:hi], MULT)
+
+        def finish_on_gpsimd(t, lo, hi, first):
+            ve = product(VALUE, t, lo, hi)
+            if first:
+                held = keep.tile([P, HALF], F32, name="held", tag="reused", align_bytes=64)
+                dst = held[:, 0:hi - lo]
             else:
-                eng, t, lo, hi = op[1:]
-                ve = product(1, t, lo, hi)
                 dst = res[t][:, lo:hi]
-                if eng == "G" and not first_pool:
-                    held = keep.tile([P, HALF], F32, name="held", tag="reused", align_bytes=64)
-                    first_pool.append(held)
-                    dst = held[:, 0:hi - lo]
-                if eng == "V":
-                    nc.vector.tensor_tensor(dst, ve, gate[t][:, lo:hi], MULT)
-                else:
-                    nc.scalar.copy(ve_sb[t][:, lo:hi], ve)
-                    nc.gpsimd.tensor_tensor(dst, ve_sb[t][:, lo:hi], gate[t][:, lo:hi], MULT)
+            nc.scalar.copy(ve_sb[t][:, lo:hi], ve)
+            nc.gpsimd.tensor_tensor(dst, ve_sb[t][:, lo:hi], gate[t][:, lo:hi], MULT)
+            if first:
                 nc.sync.dma_start(out[t * P:(t + 1) * P, lo:hi], dst)
+
+        x_planes = xT.rearrange("(p i) t -> p i t", i=PACK)
+        nc.sync.dma_start(lists[:], offs)
+        nc.sync.dma_start(wgt_sb[:, 0:HALF], wgt[:, 0:HALF])
+        nc.sync.dma_start(x_sb[0][:], x_planes[:, 0, :])
+        nc.sync.dma_start(wgt_sb[:, HALF:J], wgt[:, HALF:J])
+        for i in range(1, PACK):
+            nc.sync.dma_start(x_sb[i][:], x_planes[:, i, :])
+        for s, w in ((KEY, wk), (VALUE, wv)):
+            nc.sync.dma_start(w_sb[s][:], w.rearrange("(p i) n -> p i n", i=PACK))
+        for t, lo in PIECES:
+            nc.sync.dma_start(st_sb[t][:, lo:lo + HALF], st[t * P:(t + 1) * P, lo:lo + HALF])
+
+        for i in range(PACK - 1):
+            gather(i, 0, HALF)
+            gather(i, HALF, J)
+
+        on_scalar, on_vector = nc.scalar.copy, nc.vector.tensor_copy
+        last_plane = PACK - 1
+        mid = N // 2
+        gather(last_plane, 0, QUARTER)
+        round_x(on_scalar, 0)
+        gather(last_plane, QUARTER, HALF)
+        gather(last_plane, HALF, LAST_QUARTER)
+        round_x(on_vector, 1)
+        round_x(on_scalar, 2)
+        gather(last_plane, LAST_QUARTER, J)
+        round_w(on_scalar, KEY, mid, N)
+        round_w(on_scalar, VALUE, 0, mid)
+        round_x(on_scalar, 3)
+        quantize_x(0, HALF)
+        round_w(on_vector, KEY, 0, mid)
+        quantize_x(HALF, LAST_QUARTER)
+        quantize_w(KEY, 0, mid)
+        round_w(on_vector, VALUE, mid, N)
+        quantize_w(KEY, mid, N)
+        make_gate(PIECES[0][0], PIECES[0][1], PIECES[0][1] + HALF)
+        quantize_w(VALUE, mid, N)
+        quantize_x(LAST_QUARTER, J)
+        quantize_w(VALUE, 0, mid)
+
+        def spans(u):
+            lo = PIECES[u][1]
+            step = QUARTER if u >= FIRST_SPLIT_PIECE else HALF
+            return [(a, a + step) for a in range(lo, lo + HALF, step)]
+
+        for u, (t, lo) in enumerate(PIECES):
+            if u + 1 < len(PIECES):
+                for a, b in spans(u + 1):
+                    make_gate(PIECES[u + 1][0], a, b)
+            shared = GPSIMD_COLUMNS.get(u, 0)
+            if shared:
+                finish_on_gpsimd(t, lo, lo + shared, first=(u == min(GPSIMD_COLUMNS)))
+            last = u == len(PIECES) - 1
+            for a, b in (spans(u) if last else [(lo, lo + HALF)]):
+                if b > lo + shared:
+                    finish_on_vector(t, max(a, lo + shared), b)
+                    nc.sync.dma_start(out[t * P:(t + 1) * P, a:b], res[t][:, a:b])

from contextlib import ExitStack

import concourse.mybir as mybir

K, N, T, J = 512, 512, 2048, 1024
FLOPS = 2 * 2 * K * N * J

F32 = mybir.dt.float32
BF16 = mybir.dt.bfloat16
U32 = mybir.dt.uint32
U16 = mybir.dt.uint16
U8 = mybir.dt.uint8
FP8X4 = mybir.dt.float8_e4m3fn_x4
MULT = mybir.AluOpType.mult
TANH = mybir.ActivationFunctionType.Tanh

P = 128
PACK = 4
LIST_GROUP = 16
HALF = J // 2
QUARTER = J // 4
LAST_QUARTER = J - QUARTER
ROW_BLOCKS = N // P
KEY, VALUE = 0, 1
BANKS_EACH = 4

PIECES = [(t, h * HALF) for h in range(2) for t in range(ROW_BLOCKS)]
GPSIMD_COLUMNS = {0: HALF, 2: QUARTER, 3: QUARTER, 5: QUARTER}
FIRST_SPLIT_PIECE = len(PIECES) - 2


def tile_list_tanh_kernel(tc, xT, wgt, wk, wv, st, offs, out):
    nc = tc.nc
    with ExitStack() as ctx:
        keep = ctx.enter_context(tc.tile_pool(name="keep", bufs=1))
        psum_k = ctx.enter_context(tc.psum_pool(name="psum_k", bufs=BANKS_EACH))
        psum_v = ctx.enter_context(tc.psum_pool(name="psum_v", bufs=BANKS_EACH))

        lists = keep.tile([P, J // LIST_GROUP], U16, name="lists")
        wgt_sb = keep.tile([P, J], F32, name="wgt_sb")
        x_sb = [keep.tile([P, T], F32, name="x%d" % i) for i in range(PACK)]
        w_sb = [keep.tile([P, PACK, N], F32, name="w_sb%d" % s) for s in (KEY, VALUE)]
        st_sb = [keep.tile([P, J], F32, name="st%d" % t) for t in range(ROW_BLOCKS)]
        picked = [keep.tile([P, PACK, HALF], F32, name="picked%d" % h) for h in range(2)]
        x_bf = keep.tile([P, LAST_QUARTER, PACK], BF16, name="x_bf", align_bytes=64)
        x_last = keep.tile([P, QUARTER, PACK], BF16, name="x_last", tag="reused", align_bytes=64)
        x_codes = keep.tile([P, J], U32, name="x_codes", align_bytes=64)
        x_scales = keep.tile([P, J], U8, name="x_scales", align_bytes=64)
        w_bf = [keep.tile([P, N, PACK], BF16, name="w_bf%d" % s, align_bytes=64) for s in (KEY, VALUE)]
        w_codes = [keep.tile([P, N], U32, name="w_codes%d" % s, align_bytes=64) for s in (KEY, VALUE)]
        w_scales = [keep.tile([P, N], U8, name="w_scales%d" % s, align_bytes=64) for s in (KEY, VALUE)]
        z = [keep.tile([P, J], F32, name="z%d" % t) for t in range(ROW_BLOCKS)]
        gate = [keep.tile([P, J], F32, name="gate%d" % t) for t in range(ROW_BLOCKS)]
        ve_sb = [keep.tile([P, J], F32, name="ve%d" % t) for t in range(ROW_BLOCKS)]
        res = [keep.tile([P, J], F32, name="res%d" % t) for t in range(ROW_BLOCKS)]

        def gather(i, lo, hi):
            h, at = divmod(lo, HALF)
            nc.vector.tensor_tensor(
                picked[h][:, i, at:at + hi - lo],
                x_sb[i][:].indirect(lists[:, lo // LIST_GROUP:hi // LIST_GROUP]),
                wgt_sb[:, lo:hi],
                MULT,
            )

        def round_and_interleave(copy, dst, src):
            copy(dst.rearrange("p (c e) i -> p c i e", e=4), src.rearrange("p i (c e) -> p c i e", e=4))

        def x_grouped(lo, hi):
            return x_last[:] if lo == LAST_QUARTER else x_bf[:, lo:hi, :]

        def round_x(copy, quarter):
            lo = quarter * QUARTER
            h, at = divmod(lo, HALF)
            round_and_interleave(copy, x_grouped(lo, lo + QUARTER), picked[h][:, :, at:at + QUARTER])

        def round_w(copy, s, lo, hi):
            round_and_interleave(copy, w_bf[s][:, lo:hi, :], w_sb[s][:, :, lo:hi])

        def quantize(codes, scales, grouped):
            nc.vector.quantize_mx(
                out=codes.bitcast(FP8X4), scales=scales, in_=grouped.rearrange("p c i -> p (c i)")
            )

        def quantize_x(lo, hi):
            quantize(x_codes[:, lo:hi], x_scales[:, lo:hi], x_grouped(lo, hi))

        def quantize_w(s, lo, hi):
            quantize(w_codes[s][:, lo:hi], w_scales[s][:, lo:hi], w_bf[s][:, lo:hi, :])

        def product(s, t, lo, hi):
            pool = psum_k if s == KEY else psum_v
            acc = pool.tile([P, HALF], F32, name="acc%d" % s)
            nc.tensor.matmul_mx(
                out=acc[:, 0:hi - lo],
                lhsT=w_codes[s][:, t * P:(t + 1) * P].bitcast(FP8X4),
                lhsT_scale=w_scales[s][:, t * P:(t + 1) * P],
                rhs=x_codes[:, lo:hi].bitcast(FP8X4),
                rhs_scale=x_scales[:, lo:hi],
                start=True,
                stop=True,
            )
            return acc[:, 0:hi - lo]

        def make_gate(t, lo, hi):
            ke = product(KEY, t, lo, hi)
            nc.vector.tensor_tensor(z[t][:, lo:hi], ke, st_sb[t][:, lo:hi], MULT)
            nc.scalar.activation(gate[t][:, lo:hi], z[t][:, lo:hi], TANH)

        def finish_on_vector(t, lo, hi):
            ve = product(VALUE, t, lo, hi)
            nc.vector.tensor_tensor(res[t][:, lo:hi], ve, gate[t][:, lo:hi], MULT)

        def finish_on_gpsimd(t, lo, hi, first):
            ve = product(VALUE, t, lo, hi)
            if first:
                held = keep.tile([P, HALF], F32, name="held", tag="reused", align_bytes=64)
                dst = held[:, 0:hi - lo]
            else:
                dst = res[t][:, lo:hi]
            nc.scalar.copy(ve_sb[t][:, lo:hi], ve)
            nc.gpsimd.tensor_tensor(dst, ve_sb[t][:, lo:hi], gate[t][:, lo:hi], MULT)
            if first:
                nc.sync.dma_start(out[t * P:(t + 1) * P, lo:hi], dst)

        x_planes = xT.rearrange("(p i) t -> p i t", i=PACK)
        nc.sync.dma_start(lists[:], offs)
        nc.sync.dma_start(wgt_sb[:, 0:HALF], wgt[:, 0:HALF])
        nc.sync.dma_start(x_sb[0][:], x_planes[:, 0, :])
        nc.sync.dma_start(wgt_sb[:, HALF:J], wgt[:, HALF:J])
        for i in range(1, PACK):
            nc.sync.dma_start(x_sb[i][:], x_planes[:, i, :])
        for s, w in ((KEY, wk), (VALUE, wv)):
            nc.sync.dma_start(w_sb[s][:], w.rearrange("(p i) n -> p i n", i=PACK))
        for t, lo in PIECES:
            nc.sync.dma_start(st_sb[t][:, lo:lo + HALF], st[t * P:(t + 1) * P, lo:lo + HALF])

        for i in range(PACK - 1):
            gather(i, 0, HALF)
            gather(i, HALF, J)

        on_scalar, on_vector = nc.scalar.copy, nc.vector.tensor_copy
        last_plane = PACK - 1
        mid = N // 2
        gather(last_plane, 0, QUARTER)
        round_x(on_scalar, 0)
        gather(last_plane, QUARTER, HALF)
        gather(last_plane, HALF, LAST_QUARTER)
        round_x(on_vector, 1)
        round_x(on_scalar, 2)
        gather(last_plane, LAST_QUARTER, J)
        round_w(on_scalar, KEY, mid, N)
        round_w(on_scalar, VALUE, 0, mid)
        round_x(on_scalar, 3)
        quantize_x(0, HALF)
        round_w(on_vector, KEY, 0, mid)
        quantize_x(HALF, LAST_QUARTER)
        quantize_w(KEY, 0, mid)
        round_w(on_vector, VALUE, mid, N)
        quantize_w(KEY, mid, N)
        make_gate(PIECES[0][0], PIECES[0][1], PIECES[0][1] + HALF)
        quantize_w(VALUE, mid, N)
        quantize_x(LAST_QUARTER, J)
        quantize_w(VALUE, 0, mid)

        def spans(u):
            lo = PIECES[u][1]
            step = QUARTER if u >= FIRST_SPLIT_PIECE else HALF
            return [(a, a + step) for a in range(lo, lo + HALF, step)]

        for u, (t, lo) in enumerate(PIECES):
            if u + 1 < len(PIECES):
                for a, b in spans(u + 1):
                    make_gate(PIECES[u + 1][0], a, b)
            shared = GPSIMD_COLUMNS.get(u, 0)
            if shared:
                finish_on_gpsimd(t, lo, lo + shared, first=(u == min(GPSIMD_COLUMNS)))
            last = u == len(PIECES) - 1
            for a, b in (spans(u) if last else [(lo, lo + HALF)]):
                if b > lo + shared:
                    finish_on_vector(t, max(a, lo + shared), b)
                    nc.sync.dma_start(out[t * P:(t + 1) * P, a:b], res[t][:, a:b])
